import numpy as np
import ml_dtypes


def mxq(x, axis, fmt="e4m3"):
    dtype, down = {"e4m3": (ml_dtypes.float8_e4m3fn, 7), "e5m2": (ml_dtypes.float8_e5m2, 14)}[fmt]
    v = np.moveaxis(np.asarray(x, np.float32).astype(ml_dtypes.bfloat16).astype(np.float64), axis, -1)
    blocks = v.reshape(v.shape[:-1] + (-1, 32))
    amax = np.abs(blocks).max(-1, keepdims=True)
    byte = np.maximum(np.where(amax > 0, np.frexp(amax)[1] - 1 + 127, 0) - down, 1)
    scale = np.exp2(byte - 127.0)
    codes = (blocks / scale).astype(np.float32).astype(dtype).astype(np.float64)
    return np.moveaxis((codes * scale).reshape(v.shape), -1, axis)


WIDE = False


def mx_kscale(k, group=512):
    if not WIDE:
        return np.ones(k)
    levels = np.array([18, -18])
    if group != 512:
        return np.exp2(np.random.permutation(np.resize(levels, k // group))).repeat(group)
    if k % 512:
        return np.exp2(np.random.permutation(np.resize(levels, k // 32))).repeat(32)
    a = np.empty((k // 512, 16))
    for p in range(k // 512):
        a[p, :8] = np.random.permutation(np.resize(levels, 8))
        for g in range(8):
            far = levels[np.abs(levels - a[p, g]) >= 10]
            a[p, g + 8] = far[np.random.randint(len(far))]
    return np.exp2(a.ravel()).repeat(32)


def f64(x):
    return np.asarray(x).astype(np.float64)


E2M1 = np.array([0.0, 0.5, 1.0, 1.5, 2.0, 3.0, 4.0, 6.0, -0.0, -0.5, -1.0, -1.5, -2.0, -3.0, -4.0, -6.0])


def pack_group(w):
    k, n = w.shape
    w = f64(np.asarray(w, np.float32).astype(ml_dtypes.bfloat16)).reshape(k // 32, 32, n)
    amax = np.abs(w).max(1)
    mant, ex = np.frexp(amax / 6.0)
    byte = np.clip(np.where(amax > 0, np.where(mant > 0.5, ex, ex - 1) + 127, 1), 1, 254)
    scaled = (w * np.exp2(127.0 - byte)[:, None, :]).reshape(k, n).astype(np.float32)
    c = np.ascontiguousarray(scaled.reshape(k // 4, 4, n).transpose(0, 2, 1)).astype(ml_dtypes.float4_e2m1fn).view(np.uint8) & 0xF
    return np.ascontiguousarray((c[..., 0::2] | (c[..., 1::2] << 4)).reshape(k // 4, 2 * n)), byte.astype(np.uint8)


def unpack_group(words, scales):
    p, n = words.shape[0], scales.shape[1]
    words = np.ascontiguousarray(words).reshape(p, n, 2)
    nib = np.empty((p, n, 4), np.uint8)
    nib[..., 0::2] = words & 0xF
    nib[..., 1::2] = words >> 4
    return E2M1[nib].transpose(0, 2, 1).reshape(4 * p, n) * np.repeat(np.exp2(scales.astype(np.float64) - 127.0), 32, axis=0)


G, D, M, N = 8, 128, 128, 512


def setup_inputs():
    n = np.random.standard_normal
    s = mx_kscale(D, 0)[:, None]
    w_ = [pack_group(w) for w in n((G, D, M)) / np.sqrt(D) / s]
    return {
        "x": (n((G, D, N)) * s).astype(np.float32),
        "w_words": np.stack([w[0] for w in w_]),
        "w_scales": np.stack([w[1] for w in w_]),
    }


def reference(x, w_words, w_scales):
    xq = mxq(f64(x), 1, "e4m3")
    y = np.stack([unpack_group(w_words[g], w_scales[g]) for g in range(G)]).transpose(0, 2, 1) @ xq
    y = np.square(np.maximum(y, 0.0))
    return y

@@ -1,0 +1,139 @@
+from contextlib import ExitStack
+
+import concourse.mybir as mybir
+
+G, D, M, N = 8, 128, 128, 512
+FLOPS = 2 * G * D * M * N
+
+F32 = mybir.dt.float32
+BF16 = mybir.dt.bfloat16
+I32 = mybir.dt.int32
+U32 = mybir.dt.uint32
+U8 = mybir.dt.uint8
+FP8X4 = mybir.dt.float8_e4m3fn_x4
+FP4X4 = mybir.dt.float4_e2m1fn_x4
+ACT = mybir.ActivationFunctionType
+ALU = mybir.AluOpType
+
+P = 128
+PACK = 4
+ROWS = D // PACK
+SIDE = P // ROWS
+SETS = G // SIDE
+RUN = 4
+
+
+def tile_rows_glin_relu2_kernel(tc, x, w_words, w_scales, out):
+    nc = tc.nc
+    with ExitStack() as ctx:
+        keep = ctx.enter_context(tc.tile_pool(name="keep", bufs=1))
+        psum = ctx.enter_context(tc.psum_pool(name="psum", bufs=1))
+        ctx.enter_context(tc.manual_schedule())
+
+        xs = x.rearrange("(s c) (p j) n -> s (c p) j n", c=SIDE, j=PACK)
+        words = keep.tile([P, SETS, 2 * M], U8, align_bytes=64, name="words")
+        wsc = keep.tile([P, SETS, M], U8, align_bytes=64, name="wsc")
+        raw0 = keep.tile([P, PACK, N], F32, name="raw0")
+        raw1a = keep.tile([P, PACK, N // 2], F32, name="raw1a")
+        raw1b = keep.tile([P, PACK, N // 2], F32, name="raw1b")
+        grouped = [keep.tile([P, N, PACK], BF16, align_bytes=64, name="grouped%d" % s) for s in range(SETS)]
+        codes = [keep.tile([P, N], U32, align_bytes=64, name="codes%d" % s) for s in range(SETS)]
+        xsc = [keep.tile([P, N], U8, align_bytes=64, name="xsc%d" % s) for s in range(SETS)]
+        acc = [psum.tile([M, N], F32, name="acc%d" % g) for g in range(G)]
+        pos = [keep.tile([M, N], F32, name="pos%d" % g) for g in range(G)]
+        res = [keep.tile([M, N], F32, name="res%d" % g) for g in range(G)]
+
+        nc.vector.memset(wsc[:].bitcast(I32), 0)
+        nc.sync.dma_start(out=raw0[:], in_=xs[0])
+        nc.sync.dma_start(out=words[:].bitcast(I32), in_=w_words.rearrange("(s c) p b -> (c p) s b", c=SIDE).bitcast(I32))
+        wsv = w_scales.rearrange("(s c) f m -> c f s m", c=SIDE).bitcast(I32)
+        for c in range(SIDE):
+            nc.sync.dma_start(out=wsc[ROWS * c : ROWS * c + 4].bitcast(I32), in_=wsv[c])
+        nc.sync.dma_start(out=raw1a[:], in_=xs[1][:, :, 0 : N // 2])
+        nc.sync.dma_start(out=raw1b[:], in_=xs[1][:, :, N // 2 : N])
+
+        def views(s, raw, base, lo, hi):
+            dst = grouped[s][:, lo:hi, :].rearrange("p (c i) t -> p c t i", i=RUN)
+            src = raw[:, :, lo - base : hi - base].rearrange("p t (c i) -> p c t i", i=RUN)
+            return dst, src
+
+        def cast_v(s, raw, base, lo, hi):
+            dst, src = views(s, raw, base, lo, hi)
+            nc.vector.tensor_copy(out=dst, in_=src)
+
+        def cast_s(s, raw, base, lo, hi):
+            dst, src = views(s, raw, base, lo, hi)
+            nc.scalar.copy(out=dst, in_=src)
+
+        def quant(s, lo, hi):
+            nc.vector.quantize_mx(
+                out=codes[s][:, lo:hi].bitcast(FP8X4),
+                scales=xsc[s][:, lo:hi],
+                in_=grouped[s][:, lo:hi, :].rearrange("p n t -> p (n t)"),
+            )
+
+        def mm(s):
+            for c in range(SIDE):
+                rows = slice(ROWS * c, ROWS * (c + 1))
+                nc.tensor.matmul_mx(
+                    out=acc[SIDE * s + c][:],
+                    lhsT=words[rows, s, :].bitcast(FP4X4),
+                    lhsT_scale=wsc[rows, s, :],
+                    rhs=codes[s][rows, :].bitcast(FP8X4),
+                    rhs_scale=xsc[s][rows, :],
+                    start=True,
+                    stop=True,
+                )
+
+        def relu_s(g, lo=0, hi=N):
+            nc.scalar.activation(out=pos[g][:, lo:hi], in_=acc[g][:, lo:hi], func=ACT.Relu)
+
+        def relu_v(g, lo=0, hi=N):
+            nc.vector.tensor_scalar_max(out=pos[g][:, lo:hi], in0=acc[g][:, lo:hi], scalar1=0.0)
+
+        def sq_s(g, lo=0, hi=N):
+            nc.scalar.activation(out=res[g][:, lo:hi], in_=pos[g][:, lo:hi], func=ACT.Square)
+
+        def sq_v(g, lo=0, hi=N):
+            nc.vector.tensor_tensor(out=res[g][:, lo:hi], in0=acc[g][:, lo:hi], in1=pos[g][:, lo:hi], op=ALU.mult)
+
+        def store(g):
+            nc.sync.dma_start(out=out[g], in_=res[g][:])
+
+        cast_v(0, raw0, 0, 0, 256)
+        cast_s(0, raw0, 0, 288, 512)
+        cast_v(0, raw0, 0, 256, 288)
+        quant(0, 0, 256)
+        quant(0, 256, 512)
+        mm(0)
+        cast_v(1, raw1a, 0, 0, 256)
+        quant(1, 0, 256)
+        relu_s(0, 0, 256)
+        relu_s(0, 256, 512)
+        sq_s(0, 0, 256)
+        sq_s(0, 256, 512)
+        store(0)
+        cast_v(1, raw1b, 256, 256, 512)
+        quant(1, 256, 512)
+        mm(1)
+        relu_s(1)
+        relu_s(2)
+        sq_s(1)
+        store(1)
+        relu_v(3)
+        sq_v(2)
+        store(2)
+        sq_v(3)
+        store(3)
+        relu_s(4)
+        relu_v(7)
+        relu_s(5)
+        sq_v(4)
+        store(4)
+        relu_s(6)
+        sq_v(7)
+        store(7)
+        sq_s(6)
+        sq_v(5)
+        store(5)
+        store(6)

@@ -21,6 +21,8 @@ ROWS = D // PACK
 SIDE = P // ROWS
 SETS = G // SIDE
 RUN = 4
+HALF = N // 2
+STAGES = SETS * 2
 
 
 def tile_rows_glin_relu2_kernel(tc, x, w_words, w_scales, out):
@@ -31,109 +33,122 @@ def tile_rows_glin_relu2_kernel(tc, x, w_words, w_scales, out):
         ctx.enter_context(tc.manual_schedule())
 
         xs = x.rearrange("(s c) (p j) n -> s (c p) j n", c=SIDE, j=PACK)
+        outs = out.rearrange("(s c) m n -> s m c n", c=SIDE)
         words = keep.tile([P, SETS, 2 * M], U8, align_bytes=64, name="words")
         wsc = keep.tile([P, SETS, M], U8, align_bytes=64, name="wsc")
-        raw0 = keep.tile([P, PACK, N], F32, name="raw0")
-        raw1a = keep.tile([P, PACK, N // 2], F32, name="raw1a")
-        raw1b = keep.tile([P, PACK, N // 2], F32, name="raw1b")
-        grouped = [keep.tile([P, N, PACK], BF16, align_bytes=64, name="grouped%d" % s) for s in range(SETS)]
-        codes = [keep.tile([P, N], U32, align_bytes=64, name="codes%d" % s) for s in range(SETS)]
-        xsc = [keep.tile([P, N], U8, align_bytes=64, name="xsc%d" % s) for s in range(SETS)]
-        acc = [psum.tile([M, N], F32, name="acc%d" % g) for g in range(G)]
-        pos = [keep.tile([M, N], F32, name="pos%d" % g) for g in range(G)]
-        res = [keep.tile([M, N], F32, name="res%d" % g) for g in range(G)]
+        raw = [keep.tile([P, PACK, HALF], F32, name="raw%d" % k) for k in range(STAGES)]
+        grouped = [keep.tile([P, HALF, PACK], BF16, align_bytes=64, name="grouped%d" % k) for k in range(STAGES)]
+        codes = keep.tile([P, (STAGES + 1) * HALF], U32, align_bytes=64, name="codes")
+        xsc = keep.tile([P, (STAGES + 1) * HALF], U8, align_bytes=64, name="xsc")
+        pos = [keep.tile([M, SIDE, HALF], F32, name="pos%d" % k) for k in range(STAGES)]
+        res = [keep.tile([M, SIDE, HALF], F32, name="res%d" % k) for k in range(STAGES)]
+        acc = {}
+
+        def cols(k):
+            return slice((k % 2) * HALF, (k % 2 + 1) * HALF)
+
+        def load(k):
+            nc.sync.dma_start(out=raw[k][:], in_=xs[k // 2][:, :, cols(k)])
 
         nc.vector.memset(wsc[:].bitcast(I32), 0)
-        nc.sync.dma_start(out=raw0[:], in_=xs[0])
+        nc.vector.memset(codes[:, 0:HALF], 0)
+        nc.vector.memset(xsc[:, 0:HALF].bitcast(U32), 0)
+        load(0)
         nc.sync.dma_start(out=words[:].bitcast(I32), in_=w_words.rearrange("(s c) p b -> (c p) s b", c=SIDE).bitcast(I32))
         wsv = w_scales.rearrange("(s c) f m -> c f s m", c=SIDE).bitcast(I32)
         for c in range(SIDE):
             nc.sync.dma_start(out=wsc[ROWS * c : ROWS * c + 4].bitcast(I32), in_=wsv[c])
-        nc.sync.dma_start(out=raw1a[:], in_=xs[1][:, :, 0 : N // 2])
-        nc.sync.dma_start(out=raw1b[:], in_=xs[1][:, :, N // 2 : N])
+        for k in range(1, STAGES):
+            load(k)
 
-        def views(s, raw, base, lo, hi):
-            dst = grouped[s][:, lo:hi, :].rearrange("p (c i) t -> p c t i", i=RUN)
-            src = raw[:, :, lo - base : hi - base].rearrange("p t (c i) -> p c t i", i=RUN)
+        def views(k, lo, hi):
+            dst = grouped[k][:, lo:hi, :].rearrange("p (c i) t -> p c t i", i=RUN)
+            src = raw[k][:, :, lo:hi].rearrange("p t (c i) -> p c t i", i=RUN)
             return dst, src
 
-        def cast_v(s, raw, base, lo, hi):
-            dst, src = views(s, raw, base, lo, hi)
+        def cast_v(k, lo, hi):
+            dst, src = views(k, lo, hi)
             nc.vector.tensor_copy(out=dst, in_=src)
 
-        def cast_s(s, raw, base, lo, hi):
-            dst, src = views(s, raw, base, lo, hi)
+        def cast_s(k, lo, hi):
+            dst, src = views(k, lo, hi)
             nc.scalar.copy(out=dst, in_=src)
 
-        def quant(s, lo, hi):
+        def quant(k, lo, hi):
+            at = slice((k + 1) * HALF + lo, (k + 1) * HALF + hi)
             nc.vector.quantize_mx(
-                out=codes[s][:, lo:hi].bitcast(FP8X4),
-                scales=xsc[s][:, lo:hi],
-                in_=grouped[s][:, lo:hi, :].rearrange("p n t -> p (n t)"),
+                out=codes[:, at].bitcast(FP8X4),
+                scales=xsc[:, at],
+                in_=grouped[k][:, lo:hi, :].rearrange("p n t -> p (n t)"),
             )
 
-        def mm(s):
+        def mm(k):
+            window = slice(k * HALF, (k + 2) * HALF)
             for c in range(SIDE):
                 rows = slice(ROWS * c, ROWS * (c + 1))
+                acc[k, c] = psum.tile([M, N], F32, name="acc%d_%d" % (k, c), tag="bank%d_%d" % (k % 2, c))
                 nc.tensor.matmul_mx(
-                    out=acc[SIDE * s + c][:],
-                    lhsT=words[rows, s, :].bitcast(FP4X4),
-                    lhsT_scale=wsc[rows, s, :],
-                    rhs=codes[s][rows, :].bitcast(FP8X4),
-                    rhs_scale=xsc[s][rows, :],
+                    out=acc[k, c][:],
+                    lhsT=words[rows, k // 2, :].bitcast(FP4X4),
+                    lhsT_scale=wsc[rows, k // 2, :],
+                    rhs=codes[rows, window].bitcast(FP8X4),
+                    rhs_scale=xsc[rows, window],
                     start=True,
                     stop=True,
                 )
 
-        def relu_s(g, lo=0, hi=N):
-            nc.scalar.activation(out=pos[g][:, lo:hi], in_=acc[g][:, lo:hi], func=ACT.Relu)
+        def relu_s(k, c):
+            nc.scalar.activation(out=pos[k][:, c, :], in_=acc[k, c][:, HALF:N], func=ACT.Relu)
 
-        def relu_v(g, lo=0, hi=N):
-            nc.vector.tensor_scalar_max(out=pos[g][:, lo:hi], in0=acc[g][:, lo:hi], scalar1=0.0)
+        def relu_v(k, c):
+            nc.vector.tensor_scalar_max(out=pos[k][:, c, :], in0=acc[k, c][:, HALF:N], scalar1=0.0)
 
-        def sq_s(g, lo=0, hi=N):
-            nc.scalar.activation(out=res[g][:, lo:hi], in_=pos[g][:, lo:hi], func=ACT.Square)
+        def sq_s(k, c):
+            nc.scalar.activation(out=res[k][:, c, :], in_=pos[k][:, c, :], func=ACT.Square)
 
-        def sq_v(g, lo=0, hi=N):
-            nc.vector.tensor_tensor(out=res[g][:, lo:hi], in0=acc[g][:, lo:hi], in1=pos[g][:, lo:hi], op=ALU.mult)
+        def sq_v(k, c):
+            nc.vector.tensor_tensor(out=res[k][:, c, :], in0=pos[k][:, c, :], in1=pos[k][:, c, :], op=ALU.mult)
 
-        def store(g):
-            nc.sync.dma_start(out=out[g], in_=res[g][:])
+        def store(k, lo, hi):
+            nc.sync.dma_start(out=outs[k // 2][:, lo:hi, cols(k)], in_=res[k][:, lo:hi, :])
 
-        cast_v(0, raw0, 0, 0, 256)
-        cast_s(0, raw0, 0, 288, 512)
-        cast_v(0, raw0, 0, 256, 288)
-        quant(0, 0, 256)
-        quant(0, 256, 512)
-        mm(0)
-        cast_v(1, raw1a, 0, 0, 256)
-        quant(1, 0, 256)
-        relu_s(0, 0, 256)
-        relu_s(0, 256, 512)
-        sq_s(0, 0, 256)
-        sq_s(0, 256, 512)
-        store(0)
-        cast_v(1, raw1b, 256, 256, 512)
-        quant(1, 256, 512)
-        mm(1)
-        relu_s(1)
-        relu_s(2)
-        sq_s(1)
-        store(1)
-        relu_v(3)
-        sq_v(2)
-        store(2)
-        sq_v(3)
-        store(3)
-        relu_s(4)
-        relu_v(7)
-        relu_s(5)
-        sq_v(4)
-        store(4)
-        relu_s(6)
-        sq_v(7)
-        store(7)
-        sq_s(6)
-        sq_v(5)
-        store(5)
-        store(6)
+        def prep_shared(k):
+            cast_v(k, 0, 128)
+            cast_s(k, 160, 256)
+            cast_v(k, 128, 160)
+            quant(k, 0, 128)
+            quant(k, 128, 256)
+            mm(k)
+
+        def prep_v(k):
+            cast_v(k, 0, 128)
+            cast_v(k, 128, 256)
+            quant(k, 0, 128)
+            quant(k, 128, 256)
+
+        prep_shared(0)
+        prep_shared(1)
+        for k in range(2):
+            relu_s(k, 0)
+            relu_s(k, 1)
+            sq_s(k, 0)
+            sq_s(k, 1)
+            store(k, 0, 2)
+            relu_s(k, 2)
+            relu_s(k, 3)
+            prep_v(k + 2)
+            mm(k + 2)
+            sq_v(k, 2)
+            sq_v(k, 3)
+            store(k, 2, 4)
+        for k in range(2, STAGES):
+            relu_s(k, 0)
+            relu_s(k, 1)
+            relu_v(k, 2)
+            relu_v(k, 3)
+            sq_s(k, 0)
+            sq_v(k, 2)
+            sq_s(k, 1)
+            sq_v(k, 3)
+            store(k, 0, 2)
+            store(k, 2, 4)

@@ -114,17 +114,11 @@ def tile_rows_glin_relu2_kernel(tc, x, w_words, w_scales, out):
 
         def prep_shared(k):
             cast_v(k, 0, 128)
-            cast_s(k, 160, 256)
-            cast_v(k, 128, 160)
+            cast_s(k, 128, 256)
             quant(k, 0, 128)
             quant(k, 128, 256)
             mm(k)
 
-        def prep_v(k):
-            cast_v(k, 0, 128)
-            cast_v(k, 128, 256)
-            quant(k, 0, 128)
-            quant(k, 128, 256)
 
         prep_shared(0)
         prep_shared(1)
@@ -132,23 +126,22 @@ def tile_rows_glin_relu2_kernel(tc, x, w_words, w_scales, out):
             relu_s(k, 0)
             relu_s(k, 1)
             sq_s(k, 0)
-            sq_s(k, 1)
-            store(k, 0, 2)
+            store(k, 0, 1)
             relu_s(k, 2)
-            relu_s(k, 3)
-            prep_v(k + 2)
+            sq_s(k, 1)
+            store(k, 1, 2)
+            cast_v(k + 2, 0, HALF)
+            relu_v(k, 3)
+            quant(k + 2, 0, HALF)
             mm(k + 2)
-            sq_v(k, 2)
+            sq_s(k, 2)
+            store(k, 2, 3)
             sq_v(k, 3)
-            store(k, 2, 4)
+            store(k, 3, 4)
         for k in range(2, STAGES):
             relu_s(k, 0)
-            relu_s(k, 1)
-            relu_v(k, 2)
-            relu_v(k, 3)
-            sq_s(k, 0)
-            sq_v(k, 2)
-            sq_s(k, 1)
-            sq_v(k, 3)
-            store(k, 0, 2)
-            store(k, 2, 4)
+            for c in range(SIDE):
+                if c + 1 < SIDE:
+                    relu_s(k, c + 1)
+                sq_v(k, c)
+                store(k, c, c + 1)

@@ -120,28 +120,26 @@ def tile_rows_glin_relu2_kernel(tc, x, w_words, w_scales, out):
             mm(k)
 
 
+        def finish(k, c):
+            sq_s(k, c)
+            store(k, c, c + 1)
+
         prep_shared(0)
         prep_shared(1)
+        relu_s(0, 0)
         for k in range(2):
-            relu_s(k, 0)
-            relu_s(k, 1)
-            sq_s(k, 0)
-            store(k, 0, 1)
+            relu_v(k, 1)
             relu_s(k, 2)
-            sq_s(k, 1)
-            store(k, 1, 2)
             cast_v(k + 2, 0, HALF)
             relu_v(k, 3)
             quant(k + 2, 0, HALF)
             mm(k + 2)
-            sq_s(k, 2)
-            store(k, 2, 3)
-            sq_v(k, 3)
-            store(k, 3, 4)
+            for c in range(SIDE - 1):
+                finish(k, c)
+            if k == 0:
+                relu_s(k + 1, 0)
+            finish(k, SIDE - 1)
         for k in range(2, STAGES):
-            relu_s(k, 0)
             for c in range(SIDE):
-                if c + 1 < SIDE:
-                    relu_s(k, c + 1)
-                sq_v(k, c)
-                store(k, c, c + 1)
+                relu_v(k, c)
+                finish(k, c)

from contextlib import ExitStack

import concourse.mybir as mybir

G, D, M, N = 8, 128, 128, 512
FLOPS = 2 * G * D * M * N

F32 = mybir.dt.float32
BF16 = mybir.dt.bfloat16
I32 = mybir.dt.int32
U32 = mybir.dt.uint32
U8 = mybir.dt.uint8
FP8X4 = mybir.dt.float8_e4m3fn_x4
FP4X4 = mybir.dt.float4_e2m1fn_x4
ACT = mybir.ActivationFunctionType
ALU = mybir.AluOpType

P = 128
PACK = 4
ROWS = D // PACK
SIDE = P // ROWS
SETS = G // SIDE
RUN = 4
HALF = N // 2
STAGES = SETS * 2


def tile_rows_glin_relu2_kernel(tc, x, w_words, w_scales, out):
    nc = tc.nc
    with ExitStack() as ctx:
        keep = ctx.enter_context(tc.tile_pool(name="keep", bufs=1))
        psum = ctx.enter_context(tc.psum_pool(name="psum", bufs=1))
        ctx.enter_context(tc.manual_schedule())

        xs = x.rearrange("(s c) (p j) n -> s (c p) j n", c=SIDE, j=PACK)
        outs = out.rearrange("(s c) m n -> s m c n", c=SIDE)
        words = keep.tile([P, SETS, 2 * M], U8, align_bytes=64, name="words")
        wsc = keep.tile([P, SETS, M], U8, align_bytes=64, name="wsc")
        raw = [keep.tile([P, PACK, HALF], F32, name="raw%d" % k) for k in range(STAGES)]
        grouped = [keep.tile([P, HALF, PACK], BF16, align_bytes=64, name="grouped%d" % k) for k in range(STAGES)]
        codes = keep.tile([P, (STAGES + 1) * HALF], U32, align_bytes=64, name="codes")
        xsc = keep.tile([P, (STAGES + 1) * HALF], U8, align_bytes=64, name="xsc")
        pos = [keep.tile([M, SIDE, HALF], F32, name="pos%d" % k) for k in range(STAGES)]
        res = [keep.tile([M, SIDE, HALF], F32, name="res%d" % k) for k in range(STAGES)]
        acc = {}

        def cols(k):
            return slice((k % 2) * HALF, (k % 2 + 1) * HALF)

        def load(k):
            nc.sync.dma_start(out=raw[k][:], in_=xs[k // 2][:, :, cols(k)])

        nc.vector.memset(wsc[:].bitcast(I32), 0)
        nc.vector.memset(codes[:, 0:HALF], 0)
        nc.vector.memset(xsc[:, 0:HALF].bitcast(U32), 0)
        load(0)
        nc.sync.dma_start(out=words[:].bitcast(I32), in_=w_words.rearrange("(s c) p b -> (c p) s b", c=SIDE).bitcast(I32))
        wsv = w_scales.rearrange("(s c) f m -> c f s m", c=SIDE).bitcast(I32)
        for c in range(SIDE):
            nc.sync.dma_start(out=wsc[ROWS * c : ROWS * c + 4].bitcast(I32), in_=wsv[c])
        for k in range(1, STAGES):
            load(k)

        def views(k, lo, hi):
            dst = grouped[k][:, lo:hi, :].rearrange("p (c i) t -> p c t i", i=RUN)
            src = raw[k][:, :, lo:hi].rearrange("p t (c i) -> p c t i", i=RUN)
            return dst, src

        def cast_v(k, lo, hi):
            dst, src = views(k, lo, hi)
            nc.vector.tensor_copy(out=dst, in_=src)

        def cast_s(k, lo, hi):
            dst, src = views(k, lo, hi)
            nc.scalar.copy(out=dst, in_=src)

        def quant(k, lo, hi):
            at = slice((k + 1) * HALF + lo, (k + 1) * HALF + hi)
            nc.vector.quantize_mx(
                out=codes[:, at].bitcast(FP8X4),
                scales=xsc[:, at],
                in_=grouped[k][:, lo:hi, :].rearrange("p n t -> p (n t)"),
            )

        def mm(k):
            window = slice(k * HALF, (k + 2) * HALF)
            for c in range(SIDE):
                rows = slice(ROWS * c, ROWS * (c + 1))
                acc[k, c] = psum.tile([M, N], F32, name="acc%d_%d" % (k, c), tag="bank%d_%d" % (k % 2, c))
                nc.tensor.matmul_mx(
                    out=acc[k, c][:],
                    lhsT=words[rows, k // 2, :].bitcast(FP4X4),
                    lhsT_scale=wsc[rows, k // 2, :],
                    rhs=codes[rows, window].bitcast(FP8X4),
                    rhs_scale=xsc[rows, window],
                    start=True,
                    stop=True,
                )

        def relu_s(k, c):
            nc.scalar.activation(out=pos[k][:, c, :], in_=acc[k, c][:, HALF:N], func=ACT.Relu)

        def relu_v(k, c):
            nc.vector.tensor_scalar_max(out=pos[k][:, c, :], in0=acc[k, c][:, HALF:N], scalar1=0.0)

        def sq_s(k, c):
            nc.scalar.activation(out=res[k][:, c, :], in_=pos[k][:, c, :], func=ACT.Square)

        def sq_v(k, c):
            nc.vector.tensor_tensor(out=res[k][:, c, :], in0=pos[k][:, c, :], in1=pos[k][:, c, :], op=ALU.mult)

        def store(k, lo, hi):
            nc.sync.dma_start(out=outs[k // 2][:, lo:hi, cols(k)], in_=res[k][:, lo:hi, :])

        def prep_shared(k):
            cast_v(k, 0, 128)
            cast_s(k, 128, 256)
            quant(k, 0, 128)
            quant(k, 128, 256)
            mm(k)


        def finish(k, c):
            sq_s(k, c)
            store(k, c, c + 1)

        prep_shared(0)
        prep_shared(1)
        relu_s(0, 0)
        for k in range(2):
            relu_v(k, 1)
            relu_s(k, 2)
            cast_v(k + 2, 0, HALF)
            relu_v(k, 3)
            quant(k + 2, 0, HALF)
            mm(k + 2)
            for c in range(SIDE - 1):
                finish(k, c)
            if k == 0:
                relu_s(k + 1, 0)
            finish(k, SIDE - 1)
        for k in range(2, STAGES):
            for c in range(SIDE):
                relu_v(k, c)
                finish(k, c)
